import numpy as np
import ml_dtypes


def mxq(x, axis, fmt="e4m3"):
    dtype, down = {"e4m3": (ml_dtypes.float8_e4m3fn, 7), "e5m2": (ml_dtypes.float8_e5m2, 14)}[fmt]
    v = np.moveaxis(np.asarray(x, np.float32).astype(ml_dtypes.bfloat16).astype(np.float64), axis, -1)
    blocks = v.reshape(v.shape[:-1] + (-1, 32))
    amax = np.abs(blocks).max(-1, keepdims=True)
    byte = np.maximum(np.where(amax > 0, np.frexp(amax)[1] - 1 + 127, 0) - down, 1)
    scale = np.exp2(byte - 127.0)
    codes = (blocks / scale).astype(np.float32).astype(dtype).astype(np.float64)
    return np.moveaxis((codes * scale).reshape(v.shape), -1, axis)


WIDE = False


def mx_kscale(k):
    if not WIDE:
        return np.ones(k)
    levels = np.array([30, -30])
    if k % 512:
        return np.exp2(np.random.permutation(np.resize(levels, k // 32))).repeat(32)
    a = np.empty((k // 512, 16))
    for p in range(k // 512):
        a[p, :8] = np.random.permutation(np.resize(levels, 8))
        for g in range(8):
            far = levels[np.abs(levels - a[p, g]) >= 10]
            a[p, g + 8] = far[np.random.randint(len(far))]
    return np.exp2(a.ravel()).repeat(32)


def f64(x):
    return np.asarray(x).astype(np.float64)


def striped(idx):
    return np.tile(np.asarray(idx).reshape(-1, 16).T, (8, 1)).astype(np.uint16)


def unstriped(offs):
    return offs[:16].T.reshape(-1).astype(np.int64)


def bf(x):
    return np.asarray(x, np.float32).astype(ml_dtypes.bfloat16)


def planes(Y):
    r, m = Y.shape
    b = f64(bf(Y)).reshape(r // 32, 32, m)
    amax = np.abs(b).max(1)
    byte = np.clip(np.where(amax > 0, np.frexp(amax)[1] - 1 + 127 - 7, 1), 1, 254)
    codes = (b * np.exp2(127.0 - byte)[:, None, :]).reshape(r, m).astype(np.float32).astype(ml_dtypes.float8_e4m3fn).view(np.uint8)
    words = codes.reshape(r // 512, 128, 4, m).transpose(0, 1, 3, 2)
    return np.ascontiguousarray(words), np.ascontiguousarray(byte.astype(np.uint8).reshape(r // 512, 16, m))


K, J, N, T, V = 512, 512, 256, 1024, 1024


def setup_inputs():
    n = np.random.standard_normal
    idx = np.random.permutation(T)[:J]
    idx2 = np.random.permutation(V)[:J]
    fj = mx_kscale(J)
    return {
        "xf": (n((K, T)) * np.random.uniform(0.4, 1.6, (1, T))).astype(np.float32),
        "ca": (np.random.uniform(0.5, 1.5, (J, 1)) * fj[:, None]).astype(np.float32),
        "gt": (n((N, V)) * np.exp(0.5 * n((1, V)))).astype(np.float32),
        "rb": (np.random.uniform(0.5, 1.5, (1, J)) / fj).astype(np.float32),
        "sv": (n((N, V))).astype(np.float32),
        "old": (1.0 * n((K, N))).astype(np.float32),
        "offs": striped(idx),
        "offs2": striped(idx2),
    }


def reference(xf, ca, gt, rb, sv, old, offs, offs2):
    idx = unstriped(offs)
    idx2 = unstriped(offs2)
    xj = f64(xf)[:, idx].T
    uj = xj / (np.mean(np.abs(xj), axis=1, keepdims=True) + 0.1) * f64(ca)
    gs = f64(gt)[:, idx2] * np.maximum(f64(sv)[:, idx2], 0.0) * f64(rb)
    gj = gs.T
    ujq = mxq(uj, 0, "e5m2")
    gjq = mxq(gj, 0, "e5m2")
    w = ujq.T @ gjq
    pk1 = np.max(np.abs(w), axis=1, keepdims=True)
    y = w / (pk1 + 2.0) - 0.3 * f64(old)
    words, scales = planes(y)
    return y, words, scales

@@ -1,0 +1,179 @@
+from contextlib import ExitStack
+
+import concourse.mybir as mybir
+from concourse.masks import make_identity
+
+K, J, N, T = 512, 512, 256, 1024
+P = 128
+PACK = 4
+HALVES = N // P
+FLOPS = 2 * K * J * N
+
+F32 = mybir.dt.float32
+BF16 = mybir.dt.bfloat16
+U32 = mybir.dt.uint32
+I32 = mybir.dt.int32
+U16 = mybir.dt.uint16
+U8 = mybir.dt.uint8
+E5M2 = mybir.dt.float8_e5m2_x4
+E4M3 = mybir.dt.float8_e4m3fn_x4
+ALU = mybir.AluOpType
+ACT = mybir.ActivationFunctionType
+AX = mybir.AxisListType
+
+
+def tile_list_moment_sized_saved_rowpeaks_pl_kernel(tc, xf, ca, gt, rb, sv, old, offs, offs2, out_0, out_1, out_2):
+    nc = tc.nc
+    with ExitStack() as ctx:
+        keep = ctx.enter_context(tc.tile_pool(name="keep", bufs=1))
+        ring = ctx.enter_context(tc.tile_pool(name="ring", bufs=4))
+        psum = ctx.enter_context(tc.psum_pool(name="psum", bufs=1))
+
+        def tiles(name, count, shape, dtype):
+            return [keep.tile(shape, dtype, name=f"{name}{i}", align_bytes=64) for i in range(count)]
+
+        list_x = keep.tile([P, J // 16], U16, name="list_x")
+        list_g = keep.tile([P, J // 16], U16, name="list_g")
+        x_table = tiles("x_table", PACK, [P, T], F32)
+        s_table = tiles("s_table", HALVES, [P, T], F32)
+        g_table = tiles("g_table", HALVES, [P, T], F32)
+        ca_col = keep.tile([P, PACK], F32, name="ca_col")
+        rb_col = keep.tile([P, PACK], F32, name="rb_col")
+        old_rows = keep.tile([P, PACK, N], F32, name="old_rows")
+        ident = keep.tile([P, P], F32, name="ident")
+
+        xf_rows = xf.rearrange("(p r) t -> p r t", r=PACK)
+        nc.sync.dma_start(list_x[:], offs)
+        nc.sync.dma_start(x_table[0][:], xf_rows[:, 0, :])
+        nc.sync.dma_start(list_g[:], offs2)
+        for r in range(1, PACK):
+            nc.sync.dma_start(x_table[r][:], xf_rows[:, r, :])
+        for h in range(HALVES):
+            nc.sync.dma_start(s_table[h][:], sv[h * P : (h + 1) * P, :])
+            nc.sync.dma_start(g_table[h][:], gt[h * P : (h + 1) * P, :])
+        nc.sync.dma_start(old_rows[:], old.rearrange("(p r) n -> p r n", r=PACK))
+        make_identity(nc, ident[:])
+        nc.scalar.dma_start(ca_col[:], ca.rearrange("(q i) o -> q (i o)", i=PACK))
+        nc.scalar.dma_start(rb_col[:], rb.rearrange("o (q i) -> (o q) i", i=PACK))
+
+        x_bank = [psum.tile([P, PACK, P], F32, name=f"x_bank{r}") for r in range(PACK)]
+        g_bank = [psum.tile([P, PACK, P], F32, name=f"g_bank{h}") for h in range(HALVES)]
+
+        x_pick = tiles("x_pick", PACK, [P, PACK, P], F32)
+        mags = tiles("mags", PACK, [P, PACK], F32)
+        for r in range(PACK):
+            nc.vector.tensor_copy(x_pick[r][:].rearrange("p i q -> p q i"), x_table[r][:].indirect(list_x[:]))
+            for i in range(PACK):
+                nc.tensor.transpose(x_bank[r][:, i, :], x_pick[r][:, i, :], ident[:])
+            for i in range(PACK):
+                x_abs = ring.tile([P, P], BF16, name="x_abs")
+                nc.scalar.activation(x_abs[:], x_bank[r][:, i, :], ACT.Abs, scale=1.0 / K, accum_out=mags[r][:, i : i + 1])
+
+        s_pick = tiles("s_pick", HALVES, [P, J], F32)
+        g_pick = tiles("g_pick", HALVES, [P, J], F32)
+        part = tiles("part", PACK - 1, [P, PACK], F32)
+        nc.vector.scalar_tensor_tensor(part[0][:], mags[0][:], 0.1, mags[1][:], ALU.add, ALU.add)
+        nc.vector.tensor_tensor(part[1][:], part[0][:], mags[2][:], ALU.add)
+        nc.vector.tensor_copy(s_pick[0][:], s_table[0][:].indirect(list_g[:]))
+        nc.vector.tensor_tensor(part[2][:], part[1][:], mags[3][:], ALU.add)
+        inv = keep.tile([P, PACK], F32, name="inv")
+        nc.vector.reciprocal(inv[:], part[2][:])
+        u_gain = keep.tile([P, PACK], F32, name="u_gain")
+        nc.vector.tensor_tensor(u_gain[:], inv[:], ca_col[:], ALU.mult)
+
+        nc.scalar.activation(g_pick[0][:], g_table[0][:].indirect(list_g[:]), ACT.Copy)
+        nc.scalar.activation(s_pick[1][:], s_table[1][:].indirect(list_g[:]), ACT.Copy)
+        nc.scalar.activation(g_pick[1][:], g_table[1][:].indirect(list_g[:]), ACT.Copy)
+        decay = keep.tile([P, PACK, N], F32, name="decay")
+        nc.scalar.activation(decay[:], old_rows[:], ACT.Copy, scale=-0.3)
+
+        u_round = tiles("u_round", PACK, [P, P, PACK], BF16)
+        u_codes = tiles("u_codes", PACK, [P, P], U32)
+        u_scales = tiles("u_scales", PACK, [P, P], U8)
+        g_prod = tiles("g_prod", HALVES, [P, PACK, P], F32)
+        g_round = tiles("g_round", HALVES, [P, P, PACK], BF16)
+        g_codes = keep.tile([P, N], U32, name="g_codes", align_bytes=64)
+        g_scales = keep.tile([P, N], U8, name="g_scales", align_bytes=64)
+
+        def weigh_and_round(dst, bank, gain):
+            nc.vector.tensor_tensor(
+                dst[:], bank[:].rearrange("q i c -> q c i"), gain[:].unsqueeze(1).to_broadcast([P, P, PACK]), ALU.mult
+            )
+
+        def quantise(codes, scales, src, fmt):
+            nc.vector.quantize_mx(out=codes.bitcast(fmt), scales=scales, in_=src[:].rearrange("q c i -> q (c i)"))
+
+        def product(h):
+            nc.vector.scalar_tensor_tensor(
+                g_prod[h][:].rearrange("p i q -> p q i"),
+                s_pick[h][:].rearrange("p (q i) -> p q i", i=PACK),
+                0.0,
+                g_pick[h][:].rearrange("p (q i) -> p q i", i=PACK),
+                ALU.max,
+                ALU.mult,
+            )
+            for i in range(PACK):
+                nc.tensor.transpose(g_bank[h][:, i, :], g_prod[h][:, i, :], ident[:])
+
+        def u_step(r):
+            weigh_and_round(u_round[r], x_bank[r], u_gain)
+
+        def u_quant(r):
+            quantise(u_codes[r][:], u_scales[r][:], u_round[r], E5M2)
+
+        def g_step(h):
+            weigh_and_round(g_round[h], g_bank[h], rb_col)
+
+        def g_quant(h):
+            cols = slice(h * P, (h + 1) * P)
+            quantise(g_codes[:, cols], g_scales[:, cols], g_round[h], E5M2)
+
+        u_step(0)
+        product(0)
+        u_step(1)
+        u_quant(0)
+        g_step(0)
+        u_quant(1)
+        u_step(2)
+        g_quant(0)
+        product(1)
+        u_quant(2)
+        g_step(1)
+        u_step(3)
+        g_quant(1)
+        u_quant(3)
+
+        w_abs = tiles("w_abs", PACK, [P, N], F32)
+        peak = tiles("peak", PACK, [P, 1], F32)
+        w_gain = tiles("w_gain", PACK, [P, 1], F32)
+        y = keep.tile([P, PACK, N], F32, name="y", align_bytes=64)
+        out_rows = out_0.rearrange("(p r) n -> p r n", r=PACK)
+        w = [x_bank[r][:].rearrange("p i c -> p (i c)")[:, 0:N] for r in range(PACK)]
+        for r in range(PACK):
+            nc.tensor.matmul_mx(
+                out=w[r],
+                lhsT=u_codes[r][:].bitcast(E5M2),
+                lhsT_scale=u_scales[r][:],
+                rhs=g_codes[:].bitcast(E5M2),
+                rhs_scale=g_scales[:],
+                start=True,
+                stop=True,
+            )
+            nc.scalar.activation(w_abs[r][:], w[r], ACT.Abs)
+        for r in range(PACK):
+            nc.vector.tensor_scalar(w_abs[r][:], w_abs[r][:], 2.0, None, ALU.add, ALU.max, accum_out=peak[r][:])
+            nc.vector.reciprocal(w_gain[r][:], peak[r][:])
+            nc.vector.scalar_tensor_tensor(y[:, r, :], w[r], w_gain[r][:], decay[:, r, :], ALU.mult, ALU.add)
+            if r % 2 == 1:
+                nc.sync.dma_start(out_rows[:, r - 1 : r + 1, :], y[:, r - 1 : r + 1, :])
+
+        y_round = keep.tile([P, N, PACK], BF16, name="y_round", align_bytes=64)
+        y_codes = keep.tile([P, N], U32, name="y_codes", align_bytes=64)
+        y_scales = keep.tile([P, N], U8, name="y_scales", align_bytes=64)
+        nc.vector.tensor_copy(y_round[:], y[:].rearrange("p r n -> p n r"))
+        quantise(y_codes[:], y_scales[:], y_round, E4M3)
+        nc.sync.dma_start(out_1[0].rearrange("p c r -> p (c r)").bitcast(I32), y_codes[:].bitcast(I32))
+        scale_rows = out_2[0].bitcast(I32)
+        for quad in range(4):
+            queue = nc.scalar if quad % 2 == 0 else nc.sync
+            queue.dma_start(scale_rows[4 * quad : 4 * quad + 4, :], y_scales[32 * quad : 32 * quad + 4, :].bitcast(I32))

@@ -43,31 +43,38 @@ def tile_list_moment_sized_saved_rowpeaks_pl_kernel(tc, xf, ca, gt, rb, sv, old,
         ident = keep.tile([P, P], F32, name="ident")
 
         xf_rows = xf.rearrange("(p r) t -> p r t", r=PACK)
-        nc.sync.dma_start(list_x[:], offs)
         nc.sync.dma_start(x_table[0][:], xf_rows[:, 0, :])
-        nc.sync.dma_start(list_g[:], offs2)
+        nc.sync.dma_start(list_x[:], offs)
         for r in range(1, PACK):
             nc.sync.dma_start(x_table[r][:], xf_rows[:, r, :])
+        nc.sync.dma_start(list_g[:], offs2)
         for h in range(HALVES):
             nc.sync.dma_start(s_table[h][:], sv[h * P : (h + 1) * P, :])
             nc.sync.dma_start(g_table[h][:], gt[h * P : (h + 1) * P, :])
+            if h == 0:
+                nc.sync.dma_start(ca_col[:], ca.rearrange("(q i) o -> q (i o)", i=PACK))
+                nc.sync.dma_start(rb_col[:], rb.rearrange("o (q i) -> (o q) i", i=PACK))
         nc.sync.dma_start(old_rows[:], old.rearrange("(p r) n -> p r n", r=PACK))
         make_identity(nc, ident[:])
-        nc.scalar.dma_start(ca_col[:], ca.rearrange("(q i) o -> q (i o)", i=PACK))
-        nc.scalar.dma_start(rb_col[:], rb.rearrange("o (q i) -> (o q) i", i=PACK))
 
         x_bank = [psum.tile([P, PACK, P], F32, name=f"x_bank{r}") for r in range(PACK)]
         g_bank = [psum.tile([P, PACK, P], F32, name=f"g_bank{h}") for h in range(HALVES)]
+        spare = [psum.tile([P, PACK, P], F32, name=f"spare{h}") for h in range(2)]
 
         x_pick = tiles("x_pick", PACK, [P, PACK, P], F32)
         mags = tiles("mags", PACK, [P, PACK], F32)
         for r in range(PACK):
             nc.vector.tensor_copy(x_pick[r][:].rearrange("p i q -> p q i"), x_table[r][:].indirect(list_x[:]))
+            turned = [x_bank[r][:, i, :] for i in range(PACK)]
+            if r == PACK - 1:
+                turned = [bank[:, 0, :] for bank in spare + g_bank]
             for i in range(PACK):
-                nc.tensor.transpose(x_bank[r][:, i, :], x_pick[r][:, i, :], ident[:])
+                nc.tensor.transpose(turned[i], x_pick[r][:, i, :], ident[:])
             for i in range(PACK):
                 x_abs = ring.tile([P, P], BF16, name="x_abs")
-                nc.scalar.activation(x_abs[:], x_bank[r][:, i, :], ACT.Abs, scale=1.0 / K, accum_out=mags[r][:, i : i + 1])
+                nc.scalar.activation(x_abs[:], turned[i], ACT.Abs, scale=1.0 / K, accum_out=mags[r][:, i : i + 1])
+        for i in range(PACK):
+            nc.tensor.transpose(x_bank[PACK - 1][:, i, :], x_pick[PACK - 1][:, i, :], ident[:])
 
         s_pick = tiles("s_pick", HALVES, [P, J], F32)
         g_pick = tiles("g_pick", HALVES, [P, J], F32)
@@ -75,23 +82,36 @@ def tile_list_moment_sized_saved_rowpeaks_pl_kernel(tc, xf, ca, gt, rb, sv, old,
         nc.vector.scalar_tensor_tensor(part[0][:], mags[0][:], 0.1, mags[1][:], ALU.add, ALU.add)
         nc.vector.tensor_tensor(part[1][:], part[0][:], mags[2][:], ALU.add)
         nc.vector.tensor_copy(s_pick[0][:], s_table[0][:].indirect(list_g[:]))
-        nc.vector.tensor_tensor(part[2][:], part[1][:], mags[3][:], ALU.add)
-        inv = keep.tile([P, PACK], F32, name="inv")
-        nc.vector.reciprocal(inv[:], part[2][:])
+        nc.vector.tensor_copy(g_pick[0][:], g_table[0][:].indirect(list_g[:]))
+        ca_inv = keep.tile([P, PACK], F32, name="ca_inv")
+        nc.vector.reciprocal(ca_inv[:], ca_col[:])
+        for i in range(PACK):
+            col = slice(i, i + 1)
+            nc.vector.tensor_scalar(part[2][:, col], mags[3][:, col], part[1][:, col], ca_inv[:, col], ALU.add, ALU.mult)
         u_gain = keep.tile([P, PACK], F32, name="u_gain")
-        nc.vector.tensor_tensor(u_gain[:], inv[:], ca_col[:], ALU.mult)
+        nc.vector.reciprocal(u_gain[:], part[2][:])
 
-        nc.scalar.activation(g_pick[0][:], g_table[0][:].indirect(list_g[:]), ACT.Copy)
         nc.scalar.activation(s_pick[1][:], s_table[1][:].indirect(list_g[:]), ACT.Copy)
         nc.scalar.activation(g_pick[1][:], g_table[1][:].indirect(list_g[:]), ACT.Copy)
-        decay = keep.tile([P, PACK, N], F32, name="decay")
-        nc.scalar.activation(decay[:], old_rows[:], ACT.Copy, scale=-0.3)
 
-        u_round = tiles("u_round", PACK, [P, P, PACK], BF16)
+        u_round = [None, None, None]
+        u_round[0] = keep.tile([P, P, PACK], BF16, name="u_round0", align_bytes=64)
+        u_round[2] = keep.tile([P, P, PACK], BF16, name="u_round2", align_bytes=64)
+        u_planes = keep.tile([P, PACK, P], BF16, name="u_planes", tag="g_table1", align_bytes=64)
+        for i in range(PACK):
+            nc.scalar.activation(u_planes[:, i, :], x_bank[2][:, i, :], ACT.Copy, scale=u_gain[:, i : i + 1])
+        nc.scalar.copy(
+            u_round[2][:].rearrange("q (c e) i -> q c i e", e=4), u_planes[:].rearrange("q i (c e) -> q c i e", e=4)
+        )
+        decay = keep.tile([P, PACK, N], F32, name="decay")
+        for r in range(PACK):
+            nc.scalar.activation(decay[:, r, :], old_rows[:, r, :], ACT.Copy, scale=-0.3)
+
         u_codes = tiles("u_codes", PACK, [P, P], U32)
         u_scales = tiles("u_scales", PACK, [P, P], U8)
         g_prod = tiles("g_prod", HALVES, [P, PACK, P], F32)
         g_round = tiles("g_round", HALVES, [P, P, PACK], BF16)
+        u_round.append(g_round[HALVES - 1])
         g_codes = keep.tile([P, N], U32, name="g_codes", align_bytes=64)
         g_scales = keep.tile([P, N], U8, name="g_scales", align_bytes=64)
 
@@ -128,19 +148,19 @@ def tile_list_moment_sized_saved_rowpeaks_pl_kernel(tc, xf, ca, gt, rb, sv, old,
             cols = slice(h * P, (h + 1) * P)
             quantise(g_codes[:, cols], g_scales[:, cols], g_round[h], E5M2)
 
-        u_step(0)
         product(0)
+        u_step(0)
+        g_step(0)
+        product(1)
+        u_round[1] = keep.tile([P, P, PACK], BF16, name="u_round1", tag="s_pick1", align_bytes=64)
         u_step(1)
         u_quant(0)
-        g_step(0)
-        u_quant(1)
-        u_step(2)
         g_quant(0)
-        product(1)
-        u_quant(2)
+        u_quant(1)
         g_step(1)
-        u_step(3)
+        u_quant(2)
         g_quant(1)
+        u_step(3)
         u_quant(3)
 
         w_abs = tiles("w_abs", PACK, [P, N], F32)
@@ -170,7 +190,11 @@ def tile_list_moment_sized_saved_rowpeaks_pl_kernel(tc, xf, ca, gt, rb, sv, old,
         y_round = keep.tile([P, N, PACK], BF16, name="y_round", align_bytes=64)
         y_codes = keep.tile([P, N], U32, name="y_codes", align_bytes=64)
         y_scales = keep.tile([P, N], U8, name="y_scales", align_bytes=64)
-        nc.vector.tensor_copy(y_round[:], y[:].rearrange("p r n -> p n r"))
+        split = 160
+        dst = y_round[:].rearrange("p (c i) r -> p c r i", i=4)
+        src = y[:].rearrange("p r (c i) -> p c r i", i=4)
+        nc.vector.tensor_copy(dst[:, : split // 4], src[:, : split // 4])
+        nc.scalar.copy(dst[:, split // 4 :], src[:, split // 4 :])
         quantise(y_codes[:], y_scales[:], y_round, E4M3)
         nc.sync.dma_start(out_1[0].rearrange("p c r -> p (c r)").bitcast(I32), y_codes[:].bitcast(I32))
         scale_rows = out_2[0].bitcast(I32)

@@ -48,12 +48,12 @@ def tile_list_moment_sized_saved_rowpeaks_pl_kernel(tc, xf, ca, gt, rb, sv, old,
         for r in range(1, PACK):
             nc.sync.dma_start(x_table[r][:], xf_rows[:, r, :])
         nc.sync.dma_start(list_g[:], offs2)
-        for h in range(HALVES):
-            nc.sync.dma_start(s_table[h][:], sv[h * P : (h + 1) * P, :])
-            nc.sync.dma_start(g_table[h][:], gt[h * P : (h + 1) * P, :])
-            if h == 0:
-                nc.sync.dma_start(ca_col[:], ca.rearrange("(q i) o -> q (i o)", i=PACK))
-                nc.sync.dma_start(rb_col[:], rb.rearrange("o (q i) -> (o q) i", i=PACK))
+        nc.sync.dma_start(s_table[0][:], sv[0:P, :])
+        nc.sync.dma_start(g_table[0][:], gt[0:P, :])
+        nc.sync.dma_start(ca_col[:], ca.rearrange("(q i) o -> q (i o)", i=PACK))
+        nc.sync.dma_start(rb_col[:], rb.rearrange("o (q i) -> (o q) i", i=PACK))
+        nc.sync.dma_start(g_table[1][:], gt[P:N, :])
+        nc.sync.dma_start(s_table[1][:], sv[P:N, :])
         nc.sync.dma_start(old_rows[:], old.rearrange("(p r) n -> p r n", r=PACK))
         make_identity(nc, ident[:])
 
@@ -91,27 +91,29 @@ def tile_list_moment_sized_saved_rowpeaks_pl_kernel(tc, xf, ca, gt, rb, sv, old,
         u_gain = keep.tile([P, PACK], F32, name="u_gain")
         nc.vector.reciprocal(u_gain[:], part[2][:])
 
-        nc.scalar.activation(s_pick[1][:], s_table[1][:].indirect(list_g[:]), ACT.Copy)
         nc.scalar.activation(g_pick[1][:], g_table[1][:].indirect(list_g[:]), ACT.Copy)
-
-        u_round = [None, None, None]
-        u_round[0] = keep.tile([P, P, PACK], BF16, name="u_round0", align_bytes=64)
-        u_round[2] = keep.tile([P, P, PACK], BF16, name="u_round2", align_bytes=64)
-        u_planes = keep.tile([P, PACK, P], BF16, name="u_planes", tag="g_table1", align_bytes=64)
         for i in range(PACK):
-            nc.scalar.activation(u_planes[:, i, :], x_bank[2][:, i, :], ACT.Copy, scale=u_gain[:, i : i + 1])
-        nc.scalar.copy(
-            u_round[2][:].rearrange("q (c e) i -> q c i e", e=4), u_planes[:].rearrange("q i (c e) -> q c i e", e=4)
-        )
-        decay = keep.tile([P, PACK, N], F32, name="decay")
-        for r in range(PACK):
-            nc.scalar.activation(decay[:, r, :], old_rows[:, r, :], ACT.Copy, scale=-0.3)
+            nc.tensor.transpose(spare[0][:, i, :], g_pick[1][:, i::PACK], ident[:])
+        nc.scalar.activation(s_pick[1][:], s_table[1][:].indirect(list_g[:]), ACT.Copy)
+        g_weighed = keep.tile([P, PACK, P], F32, name="g_weighed")
+        for i in range(PACK):
+            nc.scalar.activation(g_weighed[:, i, :], spare[0][:, i, :], ACT.Copy, scale=rb_col[:, i : i + 1])
+
+        u_round = tiles("u_round", PACK, [P, P, PACK], BF16)
+        u_planes = keep.tile([P, 2, PACK, P], BF16, name="u_planes", tag="s_table1", align_bytes=64)
+        for r in (2, 3):
+            for i in range(PACK):
+                nc.scalar.activation(u_planes[:, r - 2, i, :], x_bank[r][:, i, :], ACT.Copy, scale=u_gain[:, i : i + 1])
+            nc.scalar.copy(
+                u_round[r][:].rearrange("q (c e) i -> q c i e", e=4),
+                u_planes[:, r - 2].rearrange("q i (c e) -> q c i e", e=4),
+            )
 
         u_codes = tiles("u_codes", PACK, [P, P], U32)
         u_scales = tiles("u_scales", PACK, [P, P], U8)
-        g_prod = tiles("g_prod", HALVES, [P, PACK, P], F32)
+        g_prod = tiles("g_prod", 1, [P, PACK, P], F32)
         g_round = tiles("g_round", HALVES, [P, P, PACK], BF16)
-        u_round.append(g_round[HALVES - 1])
+        u_round[1] = g_round[1]
         g_codes = keep.tile([P, N], U32, name="g_codes", align_bytes=64)
         g_scales = keep.tile([P, N], U8, name="g_scales", align_bytes=64)
 
@@ -151,21 +153,28 @@ def tile_list_moment_sized_saved_rowpeaks_pl_kernel(tc, xf, ca, gt, rb, sv, old,
         product(0)
         u_step(0)
         g_step(0)
-        product(1)
-        u_round[1] = keep.tile([P, P, PACK], BF16, name="u_round1", tag="s_pick1", align_bytes=64)
-        u_step(1)
         u_quant(0)
         g_quant(0)
-        u_quant(1)
-        g_step(1)
-        u_quant(2)
+        for i in range(PACK):
+            nc.tensor.transpose(g_bank[1][:, i, :], s_pick[1][:, i::PACK], ident[:])
+        nc.vector.scalar_tensor_tensor(
+            g_round[1][:],
+            g_bank[1][:].rearrange("q i c -> q c i"),
+            0.0,
+            g_weighed[:].rearrange("q i c -> q c i"),
+            ALU.max,
+            ALU.mult,
+        )
         g_quant(1)
-        u_step(3)
+        u_step(1)
+        u_quant(2)
+        u_quant(1)
         u_quant(3)
 
         w_abs = tiles("w_abs", PACK, [P, N], F32)
-        peak = tiles("peak", PACK, [P, 1], F32)
-        w_gain = tiles("w_gain", PACK, [P, 1], F32)
+        peak = tiles("peak", 2, [P, 2], F32)
+        w_gain = tiles("w_gain", 2, [P, 2], F32)
+        decay = keep.tile([P, PACK, N], F32, name="decay")
         y = keep.tile([P, PACK, N], F32, name="y", align_bytes=64)
         out_rows = out_0.rearrange("(p r) n -> p r n", r=PACK)
         w = [x_bank[r][:].rearrange("p i c -> p (i c)")[:, 0:N] for r in range(PACK)]
@@ -181,11 +190,30 @@ def tile_list_moment_sized_saved_rowpeaks_pl_kernel(tc, xf, ca, gt, rb, sv, old,
             )
             nc.scalar.activation(w_abs[r][:], w[r], ACT.Abs)
         for r in range(PACK):
-            nc.vector.tensor_scalar(w_abs[r][:], w_abs[r][:], 2.0, None, ALU.add, ALU.max, accum_out=peak[r][:])
-            nc.vector.reciprocal(w_gain[r][:], peak[r][:])
-            nc.vector.scalar_tensor_tensor(y[:, r, :], w[r], w_gain[r][:], decay[:, r, :], ALU.mult, ALU.add)
+            nc.scalar.activation(decay[:, r, :], old_rows[:, r, :], ACT.Copy, scale=-0.3)
+
+        def row_peak(r):
+            col = peak[r // 2][:, r % 2 : r % 2 + 1]
+            nc.vector.tensor_scalar(w_abs[r][:], w_abs[r][:], 2.0, None, ALU.add, ALU.max, accum_out=col)
+
+        def row_gains(pair):
+            nc.vector.reciprocal(w_gain[pair][:], peak[pair][:])
+
+        def row_result(r):
+            col = w_gain[r // 2][:, r % 2 : r % 2 + 1]
+            nc.vector.scalar_tensor_tensor(y[:, r, :], w[r], col, decay[:, r, :], ALU.mult, ALU.add)
             if r % 2 == 1:
                 nc.sync.dma_start(out_rows[:, r - 1 : r + 1, :], y[:, r - 1 : r + 1, :])
+
+        row_peak(0)
+        row_peak(1)
+        row_peak(2)
+        row_gains(0)
+        row_peak(3)
+        row_result(0)
+        row_gains(1)
+        for r in range(1, PACK):
+            row_result(r)
 
         y_round = keep.tile([P, N, PACK], BF16, name="y_round", align_bytes=64)
         y_codes = keep.tile([P, N], U32, name="y_codes", align_bytes=64)

@@ -26,7 +26,6 @@ def tile_list_moment_sized_saved_rowpeaks_pl_kernel(tc, xf, ca, gt, rb, sv, old,
     nc = tc.nc
     with ExitStack() as ctx:
         keep = ctx.enter_context(tc.tile_pool(name="keep", bufs=1))
-        ring = ctx.enter_context(tc.tile_pool(name="ring", bufs=4))
         psum = ctx.enter_context(tc.psum_pool(name="psum", bufs=1))
 
         def tiles(name, count, shape, dtype):
@@ -57,119 +56,118 @@ def tile_list_moment_sized_saved_rowpeaks_pl_kernel(tc, xf, ca, gt, rb, sv, old,
         nc.sync.dma_start(old_rows[:], old.rearrange("(p r) n -> p r n", r=PACK))
         make_identity(nc, ident[:])
 
-        x_bank = [psum.tile([P, PACK, P], F32, name=f"x_bank{r}") for r in range(PACK)]
+        x_bank = [psum.tile([P, PACK, P], F32, name=f"x_bank{r}") for r in range(2)]
         g_bank = [psum.tile([P, PACK, P], F32, name=f"g_bank{h}") for h in range(HALVES)]
-        spare = [psum.tile([P, PACK, P], F32, name=f"spare{h}") for h in range(2)]
+        s_bank = psum.tile([P, PACK, P], F32, name="s_bank")
+        mag_bank = [psum.tile([P, 2, P], F32, name=f"mag_bank{b}") for b in range(2)]
+
+        def turn(bank, planes):
+            for i in range(PACK):
+                nc.tensor.transpose(bank[:, i, :], planes[i], ident[:])
+
+        def weigh_planes(dst, bank, gain):
+            for i in range(PACK):
+                nc.scalar.activation(dst[:, i, :], bank[:, i, :], ACT.Copy, scale=gain[:, i : i + 1])
+
+        def quantise(codes, scales, src, fmt):
+            nc.vector.quantize_mx(out=codes.bitcast(fmt), scales=scales, in_=src)
 
         x_pick = tiles("x_pick", PACK, [P, PACK, P], F32)
-        mags = tiles("mags", PACK, [P, PACK], F32)
+        x_abs = tiles("x_abs", PACK, [P, PACK, P], F32)
         for r in range(PACK):
             nc.vector.tensor_copy(x_pick[r][:].rearrange("p i q -> p q i"), x_table[r][:].indirect(list_x[:]))
-            turned = [x_bank[r][:, i, :] for i in range(PACK)]
-            if r == PACK - 1:
-                turned = [bank[:, 0, :] for bank in spare + g_bank]
+            nc.scalar.activation(x_abs[r][:], x_pick[r][:], ACT.Abs, scale=1.0 / K)
+            if r < 2:
+                turn(x_bank[r], [x_pick[r][:, i, :] for i in range(PACK)])
             for i in range(PACK):
-                nc.tensor.transpose(turned[i], x_pick[r][:, i, :], ident[:])
-            for i in range(PACK):
-                x_abs = ring.tile([P, P], BF16, name="x_abs")
-                nc.scalar.activation(x_abs[:], turned[i], ACT.Abs, scale=1.0 / K, accum_out=mags[r][:, i : i + 1])
-        for i in range(PACK):
-            nc.tensor.transpose(x_bank[PACK - 1][:, i, :], x_pick[PACK - 1][:, i, :], ident[:])
+                nc.tensor.matmul(
+                    mag_bank[i // 2][:, i % 2, :],
+                    lhsT=x_abs[r][:, i, :],
+                    rhs=ident[:],
+                    is_transpose=True,
+                    start=(r == 0 and i % 2 == 0),
+                    stop=(r == PACK - 1 and i % 2 == 1),
+                )
 
         s_pick = tiles("s_pick", HALVES, [P, J], F32)
-        g_pick = tiles("g_pick", HALVES, [P, J], F32)
-        part = tiles("part", PACK - 1, [P, PACK], F32)
-        nc.vector.scalar_tensor_tensor(part[0][:], mags[0][:], 0.1, mags[1][:], ALU.add, ALU.add)
-        nc.vector.tensor_tensor(part[1][:], part[0][:], mags[2][:], ALU.add)
         nc.vector.tensor_copy(s_pick[0][:], s_table[0][:].indirect(list_g[:]))
-        nc.vector.tensor_copy(g_pick[0][:], g_table[0][:].indirect(list_g[:]))
-        ca_inv = keep.tile([P, PACK], F32, name="ca_inv")
-        nc.vector.reciprocal(ca_inv[:], ca_col[:])
-        for i in range(PACK):
-            col = slice(i, i + 1)
-            nc.vector.tensor_scalar(part[2][:, col], mags[3][:, col], part[1][:, col], ca_inv[:, col], ALU.add, ALU.mult)
-        u_gain = keep.tile([P, PACK], F32, name="u_gain")
-        nc.vector.reciprocal(u_gain[:], part[2][:])
-
-        nc.scalar.activation(g_pick[1][:], g_table[1][:].indirect(list_g[:]), ACT.Copy)
-        for i in range(PACK):
-            nc.tensor.transpose(spare[0][:, i, :], g_pick[1][:, i::PACK], ident[:])
+        g_pick = []
+        for h, freed in enumerate(("x_table3", "g_table0")):
+            g_pick.append(keep.tile([P, J], F32, name=f"g_pick{h}", tag=freed, align_bytes=64))
+            nc.scalar.activation(g_pick[h][:], g_table[h][:].indirect(list_g[:]), ACT.Copy)
         nc.scalar.activation(s_pick[1][:], s_table[1][:].indirect(list_g[:]), ACT.Copy)
-        g_weighed = keep.tile([P, PACK, P], F32, name="g_weighed")
-        for i in range(PACK):
-            nc.scalar.activation(g_weighed[:, i, :], spare[0][:, i, :], ACT.Copy, scale=rb_col[:, i : i + 1])
 
-        u_round = tiles("u_round", PACK, [P, P, PACK], BF16)
-        u_planes = keep.tile([P, 2, PACK, P], BF16, name="u_planes", tag="s_table1", align_bytes=64)
-        for r in (2, 3):
-            for i in range(PACK):
-                nc.scalar.activation(u_planes[:, r - 2, i, :], x_bank[r][:, i, :], ACT.Copy, scale=u_gain[:, i : i + 1])
-            nc.scalar.copy(
-                u_round[r][:].rearrange("q (c e) i -> q c i e", e=4),
-                u_planes[:, r - 2].rearrange("q i (c e) -> q c i e", e=4),
-            )
+        mag = keep.tile([P, PACK], F32, name="mag")
+        ca_inv = keep.tile([P, PACK], F32, name="ca_inv")
+        u_loss = keep.tile([P, PACK], F32, name="u_loss", align_bytes=64)
+        u_gain = keep.tile([P, PACK], F32, name="u_gain")
+        for b in range(2):
+            nc.vector.tensor_reduce(mag[:, 2 * b : 2 * b + 2], mag_bank[b][:], AX.X, ALU.add)
+            x_bank.append(psum.tile([P, PACK, P], F32, name=f"x_bank{2 + b}", tag=f"mag_bank{b}"))
+            turn(x_bank[2 + b], [x_pick[2 + b][:, i, :] for i in range(PACK)])
+        nc.vector.reciprocal(ca_inv[:], ca_col[:])
+        nc.vector.scalar_tensor_tensor(u_loss[:], mag[:], 0.1, ca_inv[:], ALU.add, ALU.mult)
+        nc.vector.reciprocal(u_gain[:], u_loss[:])
+        g_prod = keep.tile([P, PACK, P], F32, name="g_prod", tag="u_loss", align_bytes=64)
+        nc.vector.scalar_tensor_tensor(
+            g_prod[:].rearrange("p i q -> p q i"),
+            s_pick[0][:].rearrange("p (q i) -> p q i", i=PACK),
+            0.0,
+            g_pick[0][:].rearrange("p (q i) -> p q i", i=PACK),
+            ALU.max,
+            ALU.mult,
+        )
+        turn(g_bank[1], [g_pick[1][:, i::PACK] for i in range(PACK)])
+        turn(g_bank[0], [g_prod[:, i, :] for i in range(PACK)])
+        turn(s_bank, [s_pick[1][:, i::PACK] for i in range(PACK)])
 
-        u_codes = tiles("u_codes", PACK, [P, P], U32)
-        u_scales = tiles("u_scales", PACK, [P, P], U8)
-        g_prod = tiles("g_prod", 1, [P, PACK, P], F32)
+        late = keep.tile([P, 2, PACK, P], F32, name="late", tag="s_table1", align_bytes=64)
+        weigh_planes(late[:, 0], g_bank[1], rb_col)
+
+        u_round = tiles("u_round", 2, [P, 2, P, PACK], BF16)
+        u_codes = tiles("u_codes", 2, [P, 2 * P], U32)
+        u_scales = tiles("u_scales", 2, [P, 2 * P], U8)
+        weigh_planes(late[:, 1], x_bank[3], u_gain)
+        nc.scalar.copy(
+            u_round[1][:, 1].rearrange("q (c e) i -> q c i e", e=4),
+            late[:, 1].rearrange("q i (c e) -> q c i e", e=4),
+        )
+
         g_round = tiles("g_round", HALVES, [P, P, PACK], BF16)
-        u_round[1] = g_round[1]
         g_codes = keep.tile([P, N], U32, name="g_codes", align_bytes=64)
         g_scales = keep.tile([P, N], U8, name="g_scales", align_bytes=64)
 
         def weigh_and_round(dst, bank, gain):
             nc.vector.tensor_tensor(
-                dst[:], bank[:].rearrange("q i c -> q c i"), gain[:].unsqueeze(1).to_broadcast([P, P, PACK]), ALU.mult
+                dst, bank[:].rearrange("q i c -> q c i"), gain[:].unsqueeze(1).to_broadcast([P, P, PACK]), ALU.mult
             )
-
-        def quantise(codes, scales, src, fmt):
-            nc.vector.quantize_mx(out=codes.bitcast(fmt), scales=scales, in_=src[:].rearrange("q c i -> q (c i)"))
-
-        def product(h):
-            nc.vector.scalar_tensor_tensor(
-                g_prod[h][:].rearrange("p i q -> p q i"),
-                s_pick[h][:].rearrange("p (q i) -> p q i", i=PACK),
-                0.0,
-                g_pick[h][:].rearrange("p (q i) -> p q i", i=PACK),
-                ALU.max,
-                ALU.mult,
-            )
-            for i in range(PACK):
-                nc.tensor.transpose(g_bank[h][:, i, :], g_prod[h][:, i, :], ident[:])
 
         def u_step(r):
-            weigh_and_round(u_round[r], x_bank[r], u_gain)
+            weigh_and_round(u_round[r // 2][:, r % 2], x_bank[r], u_gain)
 
-        def u_quant(r):
-            quantise(u_codes[r][:], u_scales[r][:], u_round[r], E5M2)
-
-        def g_step(h):
-            weigh_and_round(g_round[h], g_bank[h], rb_col)
+        def u_quant(pair):
+            quantise(u_codes[pair][:], u_scales[pair][:], u_round[pair][:].rearrange("q r c i -> q (r c i)"), E5M2)
 
         def g_quant(h):
             cols = slice(h * P, (h + 1) * P)
-            quantise(g_codes[:, cols], g_scales[:, cols], g_round[h], E5M2)
+            quantise(g_codes[:, cols], g_scales[:, cols], g_round[h][:].rearrange("q c i -> q (c i)"), E5M2)
 
-        product(0)
         u_step(0)
-        g_step(0)
+        u_step(1)
+        weigh_and_round(g_round[0][:], g_bank[0], rb_col)
+        u_step(2)
         u_quant(0)
         g_quant(0)
-        for i in range(PACK):
-            nc.tensor.transpose(g_bank[1][:, i, :], s_pick[1][:, i::PACK], ident[:])
         nc.vector.scalar_tensor_tensor(
             g_round[1][:],
-            g_bank[1][:].rearrange("q i c -> q c i"),
+            s_bank[:].rearrange("q i c -> q c i"),
             0.0,
-            g_weighed[:].rearrange("q i c -> q c i"),
+            late[:, 0].rearrange("q i c -> q c i"),
             ALU.max,
             ALU.mult,
         )
         g_quant(1)
-        u_step(1)
-        u_quant(2)
         u_quant(1)
-        u_quant(3)
 
         w_abs = tiles("w_abs", PACK, [P, N], F32)
         peak = tiles("peak", 2, [P, 2], F32)
@@ -181,16 +179,17 @@ def tile_list_moment_sized_saved_rowpeaks_pl_kernel(tc, xf, ca, gt, rb, sv, old,
         for r in range(PACK):
             nc.tensor.matmul_mx(
                 out=w[r],
-                lhsT=u_codes[r][:].bitcast(E5M2),
-                lhsT_scale=u_scales[r][:],
+                lhsT=u_codes[r // 2][:, (r % 2) * P : (r % 2 + 1) * P].bitcast(E5M2),
+                lhsT_scale=u_scales[r // 2][:, (r % 2) * P : (r % 2 + 1) * P],
                 rhs=g_codes[:].bitcast(E5M2),
                 rhs_scale=g_scales[:],
                 start=True,
                 stop=True,
             )
             nc.scalar.activation(w_abs[r][:], w[r], ACT.Abs)
-        for r in range(PACK):
-            nc.scalar.activation(decay[:, r, :], old_rows[:, r, :], ACT.Copy, scale=-0.3)
+        for pair in range(2):
+            rows = slice(2 * pair, 2 * pair + 2)
+            nc.gpsimd.tensor_scalar(decay[:, rows, :], old_rows[:, rows, :], -0.3, 0.0, ALU.mult, ALU.add)
 
         def row_peak(r):
             col = peak[r // 2][:, r % 2 : r % 2 + 1]
@@ -223,7 +222,7 @@ def tile_list_moment_sized_saved_rowpeaks_pl_kernel(tc, xf, ca, gt, rb, sv, old,
         src = y[:].rearrange("p r (c i) -> p c r i", i=4)
         nc.vector.tensor_copy(dst[:, : split // 4], src[:, : split // 4])
         nc.scalar.copy(dst[:, split // 4 :], src[:, split // 4 :])
-        quantise(y_codes[:], y_scales[:], y_round, E4M3)
+        quantise(y_codes[:], y_scales[:], y_round[:].rearrange("p c r -> p (c r)"), E4M3)
         nc.sync.dma_start(out_1[0].rearrange("p c r -> p (c r)").bitcast(I32), y_codes[:].bitcast(I32))
         scale_rows = out_2[0].bitcast(I32)
         for quad in range(4):

@@ -187,9 +187,8 @@ def tile_list_moment_sized_saved_rowpeaks_pl_kernel(tc, xf, ca, gt, rb, sv, old,
                 stop=True,
             )
             nc.scalar.activation(w_abs[r][:], w[r], ACT.Abs)
-        for pair in range(2):
-            rows = slice(2 * pair, 2 * pair + 2)
-            nc.gpsimd.tensor_scalar(decay[:, rows, :], old_rows[:, rows, :], -0.3, 0.0, ALU.mult, ALU.add)
+        for r in range(PACK):
+            nc.scalar.activation(decay[:, r, :], old_rows[:, r, :], ACT.Copy, scale=-0.3)
 
         def row_peak(r):
             col = peak[r // 2][:, r % 2 : r % 2 + 1]

from contextlib import ExitStack

import concourse.mybir as mybir
from concourse.masks import make_identity

K, J, N, T = 512, 512, 256, 1024
P = 128
PACK = 4
HALVES = N // P
FLOPS = 2 * K * J * N

F32 = mybir.dt.float32
BF16 = mybir.dt.bfloat16
U32 = mybir.dt.uint32
I32 = mybir.dt.int32
U16 = mybir.dt.uint16
U8 = mybir.dt.uint8
E5M2 = mybir.dt.float8_e5m2_x4
E4M3 = mybir.dt.float8_e4m3fn_x4
ALU = mybir.AluOpType
ACT = mybir.ActivationFunctionType
AX = mybir.AxisListType


def tile_list_moment_sized_saved_rowpeaks_pl_kernel(tc, xf, ca, gt, rb, sv, old, offs, offs2, out_0, out_1, out_2):
    nc = tc.nc
    with ExitStack() as ctx:
        keep = ctx.enter_context(tc.tile_pool(name="keep", bufs=1))
        psum = ctx.enter_context(tc.psum_pool(name="psum", bufs=1))

        def tiles(name, count, shape, dtype):
            return [keep.tile(shape, dtype, name=f"{name}{i}", align_bytes=64) for i in range(count)]

        list_x = keep.tile([P, J // 16], U16, name="list_x")
        list_g = keep.tile([P, J // 16], U16, name="list_g")
        x_table = tiles("x_table", PACK, [P, T], F32)
        s_table = tiles("s_table", HALVES, [P, T], F32)
        g_table = tiles("g_table", HALVES, [P, T], F32)
        ca_col = keep.tile([P, PACK], F32, name="ca_col")
        rb_col = keep.tile([P, PACK], F32, name="rb_col")
        old_rows = keep.tile([P, PACK, N], F32, name="old_rows")
        ident = keep.tile([P, P], F32, name="ident")

        xf_rows = xf.rearrange("(p r) t -> p r t", r=PACK)
        nc.sync.dma_start(x_table[0][:], xf_rows[:, 0, :])
        nc.sync.dma_start(list_x[:], offs)
        for r in range(1, PACK):
            nc.sync.dma_start(x_table[r][:], xf_rows[:, r, :])
        nc.sync.dma_start(list_g[:], offs2)
        nc.sync.dma_start(s_table[0][:], sv[0:P, :])
        nc.sync.dma_start(g_table[0][:], gt[0:P, :])
        nc.sync.dma_start(ca_col[:], ca.rearrange("(q i) o -> q (i o)", i=PACK))
        nc.sync.dma_start(rb_col[:], rb.rearrange("o (q i) -> (o q) i", i=PACK))
        nc.sync.dma_start(g_table[1][:], gt[P:N, :])
        nc.sync.dma_start(s_table[1][:], sv[P:N, :])
        nc.sync.dma_start(old_rows[:], old.rearrange("(p r) n -> p r n", r=PACK))
        make_identity(nc, ident[:])

        x_bank = [psum.tile([P, PACK, P], F32, name=f"x_bank{r}") for r in range(2)]
        g_bank = [psum.tile([P, PACK, P], F32, name=f"g_bank{h}") for h in range(HALVES)]
        s_bank = psum.tile([P, PACK, P], F32, name="s_bank")
        mag_bank = [psum.tile([P, 2, P], F32, name=f"mag_bank{b}") for b in range(2)]

        def turn(bank, planes):
            for i in range(PACK):
                nc.tensor.transpose(bank[:, i, :], planes[i], ident[:])

        def weigh_planes(dst, bank, gain):
            for i in range(PACK):
                nc.scalar.activation(dst[:, i, :], bank[:, i, :], ACT.Copy, scale=gain[:, i : i + 1])

        def quantise(codes, scales, src, fmt):
            nc.vector.quantize_mx(out=codes.bitcast(fmt), scales=scales, in_=src)

        x_pick = tiles("x_pick", PACK, [P, PACK, P], F32)
        x_abs = tiles("x_abs", PACK, [P, PACK, P], F32)
        for r in range(PACK):
            nc.vector.tensor_copy(x_pick[r][:].rearrange("p i q -> p q i"), x_table[r][:].indirect(list_x[:]))
            nc.scalar.activation(x_abs[r][:], x_pick[r][:], ACT.Abs, scale=1.0 / K)
            if r < 2:
                turn(x_bank[r], [x_pick[r][:, i, :] for i in range(PACK)])
            for i in range(PACK):
                nc.tensor.matmul(
                    mag_bank[i // 2][:, i % 2, :],
                    lhsT=x_abs[r][:, i, :],
                    rhs=ident[:],
                    is_transpose=True,
                    start=(r == 0 and i % 2 == 0),
                    stop=(r == PACK - 1 and i % 2 == 1),
                )

        s_pick = tiles("s_pick", HALVES, [P, J], F32)
        nc.vector.tensor_copy(s_pick[0][:], s_table[0][:].indirect(list_g[:]))
        g_pick = []
        for h, freed in enumerate(("x_table3", "g_table0")):
            g_pick.append(keep.tile([P, J], F32, name=f"g_pick{h}", tag=freed, align_bytes=64))
            nc.scalar.activation(g_pick[h][:], g_table[h][:].indirect(list_g[:]), ACT.Copy)
        nc.scalar.activation(s_pick[1][:], s_table[1][:].indirect(list_g[:]), ACT.Copy)

        mag = keep.tile([P, PACK], F32, name="mag")
        ca_inv = keep.tile([P, PACK], F32, name="ca_inv")
        u_loss = keep.tile([P, PACK], F32, name="u_loss", align_bytes=64)
        u_gain = keep.tile([P, PACK], F32, name="u_gain")
        for b in range(2):
            nc.vector.tensor_reduce(mag[:, 2 * b : 2 * b + 2], mag_bank[b][:], AX.X, ALU.add)
            x_bank.append(psum.tile([P, PACK, P], F32, name=f"x_bank{2 + b}", tag=f"mag_bank{b}"))
            turn(x_bank[2 + b], [x_pick[2 + b][:, i, :] for i in range(PACK)])
        nc.vector.reciprocal(ca_inv[:], ca_col[:])
        nc.vector.scalar_tensor_tensor(u_loss[:], mag[:], 0.1, ca_inv[:], ALU.add, ALU.mult)
        nc.vector.reciprocal(u_gain[:], u_loss[:])
        g_prod = keep.tile([P, PACK, P], F32, name="g_prod", tag="u_loss", align_bytes=64)
        nc.vector.scalar_tensor_tensor(
            g_prod[:].rearrange("p i q -> p q i"),
            s_pick[0][:].rearrange("p (q i) -> p q i", i=PACK),
            0.0,
            g_pick[0][:].rearrange("p (q i) -> p q i", i=PACK),
            ALU.max,
            ALU.mult,
        )
        turn(g_bank[1], [g_pick[1][:, i::PACK] for i in range(PACK)])
        turn(g_bank[0], [g_prod[:, i, :] for i in range(PACK)])
        turn(s_bank, [s_pick[1][:, i::PACK] for i in range(PACK)])

        late = keep.tile([P, 2, PACK, P], F32, name="late", tag="s_table1", align_bytes=64)
        weigh_planes(late[:, 0], g_bank[1], rb_col)

        u_round = tiles("u_round", 2, [P, 2, P, PACK], BF16)
        u_codes = tiles("u_codes", 2, [P, 2 * P], U32)
        u_scales = tiles("u_scales", 2, [P, 2 * P], U8)
        weigh_planes(late[:, 1], x_bank[3], u_gain)
        nc.scalar.copy(
            u_round[1][:, 1].rearrange("q (c e) i -> q c i e", e=4),
            late[:, 1].rearrange("q i (c e) -> q c i e", e=4),
        )

        g_round = tiles("g_round", HALVES, [P, P, PACK], BF16)
        g_codes = keep.tile([P, N], U32, name="g_codes", align_bytes=64)
        g_scales = keep.tile([P, N], U8, name="g_scales", align_bytes=64)

        def weigh_and_round(dst, bank, gain):
            nc.vector.tensor_tensor(
                dst, bank[:].rearrange("q i c -> q c i"), gain[:].unsqueeze(1).to_broadcast([P, P, PACK]), ALU.mult
            )

        def u_step(r):
            weigh_and_round(u_round[r // 2][:, r % 2], x_bank[r], u_gain)

        def u_quant(pair):
            quantise(u_codes[pair][:], u_scales[pair][:], u_round[pair][:].rearrange("q r c i -> q (r c i)"), E5M2)

        def g_quant(h):
            cols = slice(h * P, (h + 1) * P)
            quantise(g_codes[:, cols], g_scales[:, cols], g_round[h][:].rearrange("q c i -> q (c i)"), E5M2)

        u_step(0)
        u_step(1)
        weigh_and_round(g_round[0][:], g_bank[0], rb_col)
        u_step(2)
        u_quant(0)
        g_quant(0)
        nc.vector.scalar_tensor_tensor(
            g_round[1][:],
            s_bank[:].rearrange("q i c -> q c i"),
            0.0,
            late[:, 0].rearrange("q i c -> q c i"),
            ALU.max,
            ALU.mult,
        )
        g_quant(1)
        u_quant(1)

        w_abs = tiles("w_abs", PACK, [P, N], F32)
        peak = tiles("peak", 2, [P, 2], F32)
        w_gain = tiles("w_gain", 2, [P, 2], F32)
        decay = keep.tile([P, PACK, N], F32, name="decay")
        y = keep.tile([P, PACK, N], F32, name="y", align_bytes=64)
        out_rows = out_0.rearrange("(p r) n -> p r n", r=PACK)
        w = [x_bank[r][:].rearrange("p i c -> p (i c)")[:, 0:N] for r in range(PACK)]
        for r in range(PACK):
            nc.tensor.matmul_mx(
                out=w[r],
                lhsT=u_codes[r // 2][:, (r % 2) * P : (r % 2 + 1) * P].bitcast(E5M2),
                lhsT_scale=u_scales[r // 2][:, (r % 2) * P : (r % 2 + 1) * P],
                rhs=g_codes[:].bitcast(E5M2),
                rhs_scale=g_scales[:],
                start=True,
                stop=True,
            )
            nc.scalar.activation(w_abs[r][:], w[r], ACT.Abs)
        for r in range(PACK):
            nc.scalar.activation(decay[:, r, :], old_rows[:, r, :], ACT.Copy, scale=-0.3)

        def row_peak(r):
            col = peak[r // 2][:, r % 2 : r % 2 + 1]
            nc.vector.tensor_scalar(w_abs[r][:], w_abs[r][:], 2.0, None, ALU.add, ALU.max, accum_out=col)

        def row_gains(pair):
            nc.vector.reciprocal(w_gain[pair][:], peak[pair][:])

        def row_result(r):
            col = w_gain[r // 2][:, r % 2 : r % 2 + 1]
            nc.vector.scalar_tensor_tensor(y[:, r, :], w[r], col, decay[:, r, :], ALU.mult, ALU.add)
            if r % 2 == 1:
                nc.sync.dma_start(out_rows[:, r - 1 : r + 1, :], y[:, r - 1 : r + 1, :])

        row_peak(0)
        row_peak(1)
        row_peak(2)
        row_gains(0)
        row_peak(3)
        row_result(0)
        row_gains(1)
        for r in range(1, PACK):
            row_result(r)

        y_round = keep.tile([P, N, PACK], BF16, name="y_round", align_bytes=64)
        y_codes = keep.tile([P, N], U32, name="y_codes", align_bytes=64)
        y_scales = keep.tile([P, N], U8, name="y_scales", align_bytes=64)
        split = 160
        dst = y_round[:].rearrange("p (c i) r -> p c r i", i=4)
        src = y[:].rearrange("p r (c i) -> p c r i", i=4)
        nc.vector.tensor_copy(dst[:, : split // 4], src[:, : split // 4])
        nc.scalar.copy(dst[:, split // 4 :], src[:, split // 4 :])
        quantise(y_codes[:], y_scales[:], y_round[:].rearrange("p c r -> p (c r)"), E4M3)
        nc.sync.dma_start(out_1[0].rearrange("p c r -> p (c r)").bitcast(I32), y_codes[:].bitcast(I32))
        scale_rows = out_2[0].bitcast(I32)
        for quad in range(4):
            queue = nc.scalar if quad % 2 == 0 else nc.sync
            queue.dma_start(scale_rows[4 * quad : 4 * quad + 4, :], y_scales[32 * quad : 32 * quad + 4, :].bitcast(I32))
